import numpy as np
import ml_dtypes


def mxq(x, axis, fmt="e4m3"):
    dtype, down = {"e4m3": (ml_dtypes.float8_e4m3fn, 7), "e5m2": (ml_dtypes.float8_e5m2, 14)}[fmt]
    v = np.moveaxis(np.asarray(x, np.float32).astype(ml_dtypes.bfloat16).astype(np.float64), axis, -1)
    blocks = v.reshape(v.shape[:-1] + (-1, 32))
    amax = np.abs(blocks).max(-1, keepdims=True)
    byte = np.maximum(np.where(amax > 0, np.frexp(amax)[1] - 1 + 127, 0) - down, 1)
    scale = np.exp2(byte - 127.0)
    codes = (blocks / scale).astype(np.float32).astype(dtype).astype(np.float64)
    return np.moveaxis((codes * scale).reshape(v.shape), -1, axis)


WIDE = False


def mx_kscale(k):
    if not WIDE:
        return np.ones(k)
    levels = np.array([10, -10, 5, -5, 0])
    if k % 512:
        return np.exp2(np.random.permutation(np.resize(levels, k // 32))).repeat(32)
    a = np.empty((k // 512, 16))
    for p in range(k // 512):
        a[p, :8] = np.random.permutation(np.resize(levels, 8))
        for g in range(8):
            far = levels[np.abs(levels - a[p, g]) >= 10]
            a[p, g + 8] = far[np.random.randint(len(far))]
    return np.exp2(a.ravel()).repeat(32)


def f64(x):
    return np.asarray(x).astype(np.float64)


def striped(idx):
    return np.tile(idx.reshape(-1, 16).T, (8, 1)).astype(np.uint16)


def unstriped(offs):
    return offs[:16].T.reshape(-1).astype(np.int64)


def pack_weight(w):
    k, n = w.shape
    w = f64(np.asarray(w, np.float32).astype(ml_dtypes.bfloat16)).reshape(k // 32, 32, n)
    amax = np.abs(w).max(1)
    byte = np.clip(np.where(amax > 0, np.frexp(amax)[1] - 1 + 127 - 7, 1), 1, 254)
    scaled = (w * np.exp2(127.0 - byte)[:, None, :]).reshape(k, n).astype(np.float32)
    words = np.ascontiguousarray(scaled.reshape(k // 512, 128, 4, n).transpose(0, 1, 3, 2)).astype(ml_dtypes.float8_e4m3fn).view(np.uint8)
    return words, np.ascontiguousarray(byte.astype(np.uint8).reshape(k // 512, 16, n))


def unpack_weight(words, scales):
    g, p, n, _ = words.shape
    vals = np.ascontiguousarray(words).view(ml_dtypes.float8_e4m3fn).astype(np.float64) * np.repeat(np.exp2(scales.astype(np.float64) - 127.0), 8, axis=1)[..., None]
    return vals.transpose(0, 1, 3, 2).reshape(g * 512, n)


E2M1 = np.array([0.0, 0.5, 1.0, 1.5, 2.0, 3.0, 4.0, 6.0, -0.0, -0.5, -1.0, -1.5, -2.0, -3.0, -4.0, -6.0])


def pack_fp4(w):
    k, n = w.shape
    w = f64(np.asarray(w, np.float32).astype(ml_dtypes.bfloat16)).reshape(k // 32, 32, n)
    amax = np.abs(w).max(1)
    mant, ex = np.frexp(amax / 6.0)
    byte = np.clip(np.where(amax > 0, np.where(mant > 0.5, ex, ex - 1) + 127, 1), 1, 254)
    scaled = (w * np.exp2(127.0 - byte)[:, None, :]).reshape(k, n).astype(np.float32)
    c = np.ascontiguousarray(scaled.reshape(k // 512, 128, 4, n).transpose(0, 1, 3, 2)).astype(ml_dtypes.float4_e2m1fn).view(np.uint8) & 0xF
    words = (c[..., 0::2] | (c[..., 1::2] << 4)).reshape(k // 512, 128, 2 * n)
    return np.ascontiguousarray(words), np.ascontiguousarray(byte.astype(np.uint8).reshape(k // 512, 16, n))


def unpack_fp4(words, scales):
    g, _, n = scales.shape
    words = np.ascontiguousarray(words).reshape(g, 128, n, 2)
    nib = np.empty((g, 128, n, 4), np.uint8)
    nib[..., 0::2] = words & 0xF
    nib[..., 1::2] = words >> 4
    vals = E2M1[nib] * np.repeat(np.exp2(scales.astype(np.float64) - 127.0), 8, axis=1)[..., None]
    return vals.transpose(0, 1, 3, 2).reshape(g * 512, n)


def relu(v):
    return np.maximum(v, 0.0)


def sigmoid(v):
    return 1.0 / (1.0 + np.exp(-np.maximum(v, -700.0)))


K, T, S, N, H = 1024, 1024, 512, 256, 512


def setup_inputs():
    n = np.random.standard_normal
    s = mx_kscale(K)[:, None]
    u = mx_kscale(H)
    packed_xT = pack_weight(n((K, T)) * s)
    packed_w1 = pack_fp4(n((K, H)) / np.sqrt(K) / s)
    packed_w2 = pack_fp4(n((K, H)) / np.sqrt(K) / s)
    packed_w3 = pack_fp4(n((H, N)) / np.sqrt(H) / u[:, None])
    return {
        "x_words": packed_xT[0],
        "x_scales": packed_xT[1],
        "w1_words": packed_w1[0],
        "w1_scales": packed_w1[1],
        "w2_words": packed_w2[0],
        "w2_scales": packed_w2[1],
        "load": (np.random.uniform(0.5, 1.5, (H, S))).astype(np.float32),
        "unit": (np.random.uniform(0.6, 1.4, (H, 1)) * u[:, None]).astype(np.float32),
        "w3_words": packed_w3[0],
        "w3_scales": packed_w3[1],
        "offs": striped(np.random.permutation(T)[:S]),
        "nxt": striped(np.random.permutation(S)),
    }


def reference(x_words, x_scales, w1_words, w1_scales, w2_words, w2_scales, load, unit, w3_words, w3_scales, offs, nxt):
    xq = unpack_weight(x_words, x_scales)[:, unstriped(offs)]
    y = unpack_fp4(w1_words, w1_scales).T @ xq
    tr = unpack_fp4(w2_words, w2_scales).T @ xq
    speed = np.exp(0.8 * np.tanh(tr))
    dwell = (np.log(np.exp(y) + 1.0)) / (speed + 0.3)
    dnx = dwell[:, unstriped(nxt)]
    jam = relu(dnx - dwell)
    flow = f64(load) / (dwell + jam + 0.5)
    fs = flow * speed
    hid = f64(unit) * (fs * (sigmoid(y[:, unstriped(nxt)])))
    return unpack_fp4(w3_words, w3_scales).T @ mxq(hid, 0, "e4m3")

@@ -1,0 +1,215 @@
+from contextlib import ExitStack
+
+import concourse.mybir as mybir
+
+K, T, S, N, H = 1024, 1024, 512, 256, 512
+FLOPS = 2 * K * H * S * 2 + 2 * H * N * S
+
+F32 = mybir.dt.float32
+BF16 = mybir.dt.bfloat16
+I32 = mybir.dt.int32
+U32 = mybir.dt.uint32
+U16 = mybir.dt.uint16
+U8 = mybir.dt.uint8
+FP8X4 = mybir.dt.float8_e4m3fn_x4
+FP4X4 = mybir.dt.float4_e2m1fn_x4
+ACT = mybir.ActivationFunctionType
+ALU = mybir.AluOpType
+
+P = 128
+PACK = 4
+PASSES = K // (P * PACK)
+HALF = S // 2
+CHUNK = 128
+LN_03 = -1.2039728043259361
+TINY = 2.0 ** -60
+ON_VECTOR = ((3, 1),)
+
+
+def tile_picked_yetasc_gate_p_kernel(
+    tc, x_words, x_scales, w1_words, w1_scales, w2_words, w2_scales, load, unit, w3_words, w3_scales, offs, nxt, out
+):
+    nc = tc.nc
+    with ExitStack() as ctx:
+        sb = ctx.enter_context(tc.tile_pool(name="sb", bufs=1))
+        ps = ctx.enter_context(tc.psum_pool(name="ps", bufs=1))
+
+        def load_scale_rows(queue, plane, rows, quadrants):
+            for q in quadrants:
+                queue.dma_start(
+                    out=plane[32 * q : 32 * q + 4, :, :].bitcast(I32),
+                    in_=rows[:, 4 * q : 4 * q + 4, :].rearrange("o r n -> r o n").bitcast(I32),
+                )
+
+        offs_sb = sb.tile([P, S // 16], U16, name="offs_sb")
+        nxt_sb = sb.tile([P, S // 16], U16, name="nxt_sb")
+        x_bytes = sb.tile([P, PASSES, T], U8, name="x_bytes", align_bytes=64)
+        x_table = sb.tile([P, PASSES, T], U32, name="x_table", align_bytes=64)
+        ws_raw = sb.tile([P, 2, PASSES, H], U8, name="ws_raw", align_bytes=64)
+        w3_sb = sb.tile([P, 2 * N], U8, name="w3_sb", align_bytes=64)
+        w3s_sb = sb.tile([P, 1, N], U8, name="w3s_sb", align_bytes=64)
+        load_sb = sb.tile([P, PACK, S], F32, name="load_sb")
+        unit_sb = sb.tile([P, PACK], F32, name="unit_sb")
+
+        nc.vector.memset(x_bytes[:, 0, :].bitcast(I32), 0)
+        nc.gpsimd.memset(x_bytes[:, 1, :].bitcast(I32), 0)
+        nc.vector.memset(ws_raw[:, 0].bitcast(I32), 0)
+        nc.gpsimd.memset(ws_raw[:, 1].bitcast(I32), 0)
+        nc.gpsimd.memset(w3s_sb[:].bitcast(I32), 0)
+
+        def load_w(words, name):
+            w_raw = sb.tile([P, PASSES, 2 * H], U8, name=name, align_bytes=64)
+            nc.sync.dma_start(out=w_raw[:].bitcast(I32), in_=words.rearrange("o p n -> p o n").bitcast(I32))
+            return w_raw
+
+        xg = [sb.tile([P, S], U32, name="xg%d" % o, align_bytes=64) for o in range(PASSES)]
+        xs = [sb.tile([P, S], U8, name="xs%d" % o, align_bytes=64) for o in range(PASSES)]
+        wd = sb.tile([P, 2, PACK, PASSES, 2 * P], U8, name="wd", tag="wd", align_bytes=64)
+        wsd = sb.tile([P, PACK, 2, PASSES, P], U8, name="wsd", align_bytes=64)
+
+        def half_list(lst, h):
+            return lst[:, h * (HALF // 16) : (h + 1) * (HALF // 16)]
+
+        def deal_words(w_raw, i, t):
+            src = w_raw[:].bitcast(U16).rearrange("p o (m t) -> p o t m", t=PACK)
+            nc.scalar.copy(out=wd[:, i, t, :, :].bitcast(U16), in_=src[:, :, t, :])
+
+        def deal_bytes(t):
+            src = ws_raw[:].rearrange("p i o (m t) -> p t i o m", t=PACK)
+            nc.gpsimd.tensor_copy(out=wsd[:, t], in_=src[:, t])
+
+        nc.sync.dma_start(offs_sb[:], offs)
+        w1_raw = load_w(w1_words, "w1_raw")
+        load_scale_rows(nc.sync, x_bytes, x_scales, (0, 1))
+        load_scale_rows(nc.scalar, x_bytes, x_scales, (2, 3))
+        nc.sync.dma_start(out=x_table[:].bitcast(I32), in_=x_words.rearrange("o p n t -> p o (n t)").bitcast(I32))
+        for i, rows in enumerate((w1_scales, w2_scales)):
+            load_scale_rows(nc.sync, ws_raw[:, i], rows, range(3))
+            load_scale_rows(nc.gpsimd, ws_raw[:, i], rows, (3,))
+        w2_raw = load_w(w2_words, "w2_raw")
+        nc.sync.dma_start(nxt_sb[:], nxt)
+        load_rows = load.rearrange("(p t) j -> p t j", t=PACK)
+        nc.sync.dma_start(out=unit_sb[:], in_=unit.rearrange("(p t) o -> p (t o)", t=PACK))
+        for pair in range(2):
+            nc.sync.dma_start(out=load_sb[:, 2 * pair : 2 * pair + 2, :], in_=load_rows[:, 2 * pair : 2 * pair + 2, :])
+        nc.sync.dma_start(out=w3_sb[:].bitcast(I32), in_=w3_words[0].bitcast(I32))
+        load_scale_rows(nc.sync, w3s_sb, w3_scales, range(4))
+
+        for t in range(PACK):
+            deal_words(w1_raw, 0, t)
+        for t in range(PACK):
+            deal_words(w2_raw, 1, t)
+        for o in range(PASSES):
+            nc.vector.tensor_copy(xs[o][:], x_bytes[:, o, :].indirect(offs_sb[:]))
+        for h in range(2):
+            for o in range(PASSES):
+                nc.vector.tensor_copy(xg[o][:, h * HALF : (h + 1) * HALF], x_table[:, o, :].indirect(half_list(offs_sb, h)))
+        for t in range(PACK):
+            deal_bytes(t)
+
+        sig = [sb.tile([P, S], F32, name="sig%d" % t) for t in range(PACK)]
+        th = sb.tile([P, PACK, S], F32, name="th")
+        rate = sb.tile([P, PACK, S], F32, name="rate")
+        banks = {}
+
+        def open_bank(i, t):
+            banks[(i, t)] = ps.tile([P, S], F32, name="bank%d%d" % (i, t), tag="bank%d" % (t + i))
+
+        def one_pass(i, t, o, cols):
+            nc.tensor.matmul_mx(
+                out=banks[(i, t)][:, cols],
+                lhsT=wd[:, i, t, o, :].bitcast(FP4X4),
+                lhsT_scale=wsd[:, t, i, o, :],
+                rhs=xg[o][:, cols].bitcast(FP8X4),
+                rhs_scale=xs[o][:, cols],
+                start=(o == 0),
+                stop=(o == PASSES - 1),
+            )
+
+        def sigmoid_y(t):
+            nc.scalar.activation(out=sig[t][:], in_=banks[(0, t)][:], func=ACT.Sigmoid)
+
+        def tanh_tr(t):
+            nc.scalar.activation(out=th[:, t, :], in_=banks[(1, t)][:], func=ACT.Tanh)
+
+        def rate_of(t):
+            nc.scalar.activation(out=rate[:, t, :], in_=th[:, t, :], func=ACT.Sigmoid, scale=-0.8, bias=LN_03)
+
+        open_bank(0, 0)
+        open_bank(1, 0)
+        for h in range(2):
+            for i in range(2):
+                for o in range(PASSES):
+                    one_pass(i, 0, o, slice(h * HALF, (h + 1) * HALF))
+        sigmoid_y(0)
+        tanh_tr(0)
+        for t in range(1, PACK):
+            for i in (1, 0):
+                open_bank(i, t)
+                for o in range(PASSES):
+                    one_pass(i, t, o, slice(0, S))
+            tanh_tr(t)
+            rate_of(t - 1)
+            sigmoid_y(t)
+        rate_of(PACK - 1)
+
+        lsig = sb.tile([P, PACK, S], F32, name="lsig", tag="wd", align_bytes=64)
+        soft = sb.tile([P, PACK, S], F32, name="soft")
+        dw = [sb.tile([P, S], F32, name="dw%d" % t) for t in range(PACK)]
+        dwn = sb.tile([P, PACK, S], F32, name="dwn")
+        slow = sb.tile([P, PACK, S], F32, name="slow")
+        lw = sb.tile([P, PACK, S], F32, name="lw")
+        expo = sb.tile([P, PACK, S], F32, name="expo")
+        sign_ = sb.tile([P, PACK, S], F32, name="sign_")
+        gain = sb.tile([P, PACK, S], F32, name="gain")
+
+        for t in range(PACK):
+            nc.scalar.activation(out=lsig[:, t, :], in_=sig[t][:], func=ACT.Ln, bias=TINY)
+        for t in range(PACK):
+            nc.vector.tensor_tensor(soft[:, t, :], lsig[:, t, :], banks[(0, t)][:], ALU.subtract)
+            nc.vector.tensor_tensor(dw[t][:], soft[:, t, :], rate[:, t, :], ALU.mult)
+            for h in range(2):
+                cols = slice(h * HALF, (h + 1) * HALF)
+                if (t, h) in ON_VECTOR:
+                    nc.vector.tensor_copy(dwn[:, t, cols], dw[t][:].indirect(half_list(nxt_sb, h)))
+                else:
+                    nc.scalar.activation(out=dwn[:, t, cols], in_=dw[t][:].indirect(half_list(nxt_sb, h)), func=ACT.Copy)
+        for t in range(PACK):
+            nc.vector.scalar_tensor_tensor(slow[:, t, :], dwn[:, t, :], 0.0, dw[t][:], ALU.min, ALU.min)
+            nc.scalar.activation(out=lw[:, t, :], in_=slow[:, t, :], func=ACT.Ln, scale=-1.0 / 0.3, bias=0.5)
+        for t in range(PACK):
+            nc.vector.scalar_tensor_tensor(expo[:, t, :], th[:, t, :], 0.8, lw[:, t, :], ALU.mult, ALU.subtract)
+        for t in range(PACK):
+            for h in range(2):
+                cols = slice(h * HALF, (h + 1) * HALF)
+                nc.vector.tensor_copy(sign_[:, t, cols], sig[t][:].indirect(half_list(nxt_sb, h)))
+            nc.vector.scalar_tensor_tensor(gain[:, t, :], sign_[:, t, :], unit_sb[:, t : t + 1], load_sb[:, t, :], ALU.mult, ALU.mult)
+
+        out_rows = out.rearrange("(u p) j -> p u j", p=P)
+        for c in range(S // CHUNK):
+            cols = slice(c * CHUNK, (c + 1) * CHUNK)
+            ex = sb.tile([P, PACK, CHUNK], F32, name="ex%d" % c)
+            hid = sb.tile([P, PACK, CHUNK], BF16, name="hid%d" % c)
+            woven = sb.tile([P, CHUNK, PACK], BF16, name="woven%d" % c, align_bytes=64)
+            codes = sb.tile([P, CHUNK], U32, name="codes%d" % c, align_bytes=64)
+            cs = sb.tile([P, CHUNK], U8, name="cs%d" % c, align_bytes=64)
+            res = sb.tile([P, 2, CHUNK], F32, name="res%d" % c)
+            acc = ps.tile([P, 2, CHUNK], F32, name="acc%d" % c, tag="bank%d" % (PACK + c))
+            nc.scalar.activation(out=ex[:], in_=expo[:, :, cols], func=ACT.Exp)
+            nc.vector.tensor_tensor(hid[:], ex[:], gain[:, :, cols], ALU.mult)
+            nc.vector.tensor_copy(
+                out=woven[:].rearrange("p (c i) t -> p c t i", i=4), in_=hid[:].rearrange("p t (c i) -> p c t i", i=4)
+            )
+            nc.vector.quantize_mx(out=codes[:].bitcast(FP8X4), scales=cs[:], in_=woven[:].rearrange("p j t -> p (j t)"))
+            for u in range(2):
+                nc.tensor.matmul_mx(
+                    out=acc[:, u, :],
+                    lhsT=w3_sb[:, u * 2 * P : (u + 1) * 2 * P].bitcast(FP4X4),
+                    lhsT_scale=w3s_sb[:, 0, u * P : (u + 1) * P],
+                    rhs=codes[:].bitcast(FP8X4),
+                    rhs_scale=cs[:],
+                    start=True,
+                    stop=True,
+                )
+            nc.scalar.copy(out=res[:], in_=acc[:])
+            nc.sync.dma_start(out=out_rows[:, :, cols], in_=res[:])

@@ -82,11 +82,11 @@ def tile_picked_yetasc_gate_p_kernel(
         w1_raw = load_w(w1_words, "w1_raw")
         load_scale_rows(nc.sync, x_bytes, x_scales, (0, 1))
         load_scale_rows(nc.scalar, x_bytes, x_scales, (2, 3))
+        w2_raw = load_w(w2_words, "w2_raw")
         nc.sync.dma_start(out=x_table[:].bitcast(I32), in_=x_words.rearrange("o p n t -> p o (n t)").bitcast(I32))
         for i, rows in enumerate((w1_scales, w2_scales)):
             load_scale_rows(nc.sync, ws_raw[:, i], rows, range(3))
             load_scale_rows(nc.gpsimd, ws_raw[:, i], rows, (3,))
-        w2_raw = load_w(w2_words, "w2_raw")
         nc.sync.dma_start(nxt_sb[:], nxt)
         load_rows = load.rearrange("(p t) j -> p t j", t=PACK)
         nc.sync.dma_start(out=unit_sb[:], in_=unit.rearrange("(p t) o -> p (t o)", t=PACK))
@@ -110,48 +110,42 @@ def tile_picked_yetasc_gate_p_kernel(
         sig = [sb.tile([P, S], F32, name="sig%d" % t) for t in range(PACK)]
         th = sb.tile([P, PACK, S], F32, name="th")
         rate = sb.tile([P, PACK, S], F32, name="rate")
-        banks = {}
+        y_ps = {}
 
-        def open_bank(i, t):
-            banks[(i, t)] = ps.tile([P, S], F32, name="bank%d%d" % (i, t), tag="bank%d" % (t + i))
+        def product(dst, i, t, cols):
+            for o in range(PASSES):
+                nc.tensor.matmul_mx(
+                    out=dst,
+                    lhsT=wd[:, i, t, o, :].bitcast(FP4X4),
+                    lhsT_scale=wsd[:, t, i, o, :],
+                    rhs=xg[o][:, cols].bitcast(FP8X4),
+                    rhs_scale=xs[o][:, cols],
+                    start=(o == 0),
+                    stop=(o == PASSES - 1),
+                )
 
-        def one_pass(i, t, o, cols):
-            nc.tensor.matmul_mx(
-                out=banks[(i, t)][:, cols],
-                lhsT=wd[:, i, t, o, :].bitcast(FP4X4),
-                lhsT_scale=wsd[:, t, i, o, :],
-                rhs=xg[o][:, cols].bitcast(FP8X4),
-                rhs_scale=xs[o][:, cols],
-                start=(o == 0),
-                stop=(o == PASSES - 1),
-            )
+        def rate_of(t, cols):
+            nc.scalar.activation(out=rate[:, t, cols], in_=th[:, t, cols], func=ACT.Sigmoid, scale=-0.8, bias=LN_03)
 
-        def sigmoid_y(t):
-            nc.scalar.activation(out=sig[t][:], in_=banks[(0, t)][:], func=ACT.Sigmoid)
-
-        def tanh_tr(t):
-            nc.scalar.activation(out=th[:, t, :], in_=banks[(1, t)][:], func=ACT.Tanh)
-
-        def rate_of(t):
-            nc.scalar.activation(out=rate[:, t, :], in_=th[:, t, :], func=ACT.Sigmoid, scale=-0.8, bias=LN_03)
-
-        open_bank(0, 0)
-        open_bank(1, 0)
         for h in range(2):
+            cols = slice(h * HALF, (h + 1) * HALF)
+            bank = ps.tile([P, 2, HALF], F32, name="first%d" % h, tag="first%d" % h)
             for i in range(2):
-                for o in range(PASSES):
-                    one_pass(i, 0, o, slice(h * HALF, (h + 1) * HALF))
-        sigmoid_y(0)
-        tanh_tr(0)
+                product(bank[:, i, :], i, 0, cols)
+            y_ps[(0, h)] = bank[:, 0, :]
+            nc.scalar.activation(out=sig[0][:, cols], in_=bank[:, 0, :], func=ACT.Sigmoid)
+            nc.scalar.activation(out=th[:, 0, cols], in_=bank[:, 1, :], func=ACT.Tanh)
+            rate_of(0, cols)
         for t in range(1, PACK):
-            for i in (1, 0):
-                open_bank(i, t)
-                for o in range(PASSES):
-                    one_pass(i, t, o, slice(0, S))
-            tanh_tr(t)
-            rate_of(t - 1)
-            sigmoid_y(t)
-        rate_of(PACK - 1)
+            tr_bank = ps.tile([P, S], F32, name="tr_bank%d" % t, tag="tr_bank%d" % t)
+            y_bank = ps.tile([P, S], F32, name="y_bank%d" % t, tag="y_bank%d" % t)
+            product(tr_bank[:], 1, t, slice(0, S))
+            product(y_bank[:], 0, t, slice(0, S))
+            for h in range(2):
+                y_ps[(t, h)] = y_bank[:, h * HALF : (h + 1) * HALF]
+            nc.scalar.activation(out=th[:, t, :], in_=tr_bank[:], func=ACT.Tanh)
+            nc.scalar.activation(out=sig[t][:], in_=y_bank[:], func=ACT.Sigmoid)
+            rate_of(t, slice(0, S))
 
         lsig = sb.tile([P, PACK, S], F32, name="lsig", tag="wd", align_bytes=64)
         soft = sb.tile([P, PACK, S], F32, name="soft")
@@ -166,8 +160,12 @@ def tile_picked_yetasc_gate_p_kernel(
         for t in range(PACK):
             nc.scalar.activation(out=lsig[:, t, :], in_=sig[t][:], func=ACT.Ln, bias=TINY)
         for t in range(PACK):
-            nc.vector.tensor_tensor(soft[:, t, :], lsig[:, t, :], banks[(0, t)][:], ALU.subtract)
-            nc.vector.tensor_tensor(dw[t][:], soft[:, t, :], rate[:, t, :], ALU.mult)
+            for h in range(2):
+                cols = slice(h * HALF, (h + 1) * HALF)
+                nc.vector.tensor_tensor(soft[:, t, cols], lsig[:, t, cols], y_ps[(t, h)], ALU.subtract)
+            for h in range(2):
+                cols = slice(h * HALF, (h + 1) * HALF)
+                nc.vector.tensor_tensor(dw[t][:, cols], soft[:, t, cols], rate[:, t, cols], ALU.mult)
             for h in range(2):
                 cols = slice(h * HALF, (h + 1) * HALF)
                 if (t, h) in ON_VECTOR:
@@ -194,12 +192,10 @@ def tile_picked_yetasc_gate_p_kernel(
             codes = sb.tile([P, CHUNK], U32, name="codes%d" % c, align_bytes=64)
             cs = sb.tile([P, CHUNK], U8, name="cs%d" % c, align_bytes=64)
             res = sb.tile([P, 2, CHUNK], F32, name="res%d" % c)
-            acc = ps.tile([P, 2, CHUNK], F32, name="acc%d" % c, tag="bank%d" % (PACK + c))
+            acc = ps.tile([P, 2, CHUNK], F32, name="acc%d" % c, tag="tr_bank%d" % c if c else "first0")
             nc.scalar.activation(out=ex[:], in_=expo[:, :, cols], func=ACT.Exp)
             nc.vector.tensor_tensor(hid[:], ex[:], gain[:, :, cols], ALU.mult)
-            nc.vector.tensor_copy(
-                out=woven[:].rearrange("p (c i) t -> p c t i", i=4), in_=hid[:].rearrange("p t (c i) -> p c t i", i=4)
-            )
+            nc.vector.tensor_copy(out=woven[:].rearrange("p (c i) t -> p c t i", i=4), in_=hid[:].rearrange("p t (c i) -> p c t i", i=4))
             nc.vector.quantize_mx(out=codes[:].bitcast(FP8X4), scales=cs[:], in_=woven[:].rearrange("p j t -> p (j t)"))
             for u in range(2):
                 nc.tensor.matmul_mx(

@@ -187,15 +187,18 @@ def tile_picked_yetasc_gate_p_kernel(
         for c in range(S // CHUNK):
             cols = slice(c * CHUNK, (c + 1) * CHUNK)
             ex = sb.tile([P, PACK, CHUNK], F32, name="ex%d" % c)
-            hid = sb.tile([P, PACK, CHUNK], BF16, name="hid%d" % c)
             woven = sb.tile([P, CHUNK, PACK], BF16, name="woven%d" % c, align_bytes=64)
             codes = sb.tile([P, CHUNK], U32, name="codes%d" % c, align_bytes=64)
             cs = sb.tile([P, CHUNK], U8, name="cs%d" % c, align_bytes=64)
             res = sb.tile([P, 2, CHUNK], F32, name="res%d" % c)
             acc = ps.tile([P, 2, CHUNK], F32, name="acc%d" % c, tag="tr_bank%d" % c if c else "first0")
             nc.scalar.activation(out=ex[:], in_=expo[:, :, cols], func=ACT.Exp)
-            nc.vector.tensor_tensor(hid[:], ex[:], gain[:, :, cols], ALU.mult)
-            nc.vector.tensor_copy(out=woven[:].rearrange("p (c i) t -> p c t i", i=4), in_=hid[:].rearrange("p t (c i) -> p c t i", i=4))
+            nc.vector.tensor_tensor(
+                woven[:].rearrange("p (c i) t -> p c t i", i=4),
+                ex[:].rearrange("p t (c i) -> p c t i", i=4),
+                gain[:, :, cols].rearrange("p t (c i) -> p c t i", i=4),
+                ALU.mult,
+            )
             nc.vector.quantize_mx(out=codes[:].bitcast(FP8X4), scales=cs[:], in_=woven[:].rearrange("p j t -> p (j t)"))
             for u in range(2):
                 nc.tensor.matmul_mx(

from contextlib import ExitStack

import concourse.mybir as mybir

K, T, S, N, H = 1024, 1024, 512, 256, 512
FLOPS = 2 * K * H * S * 2 + 2 * H * N * S

F32 = mybir.dt.float32
BF16 = mybir.dt.bfloat16
I32 = mybir.dt.int32
U32 = mybir.dt.uint32
U16 = mybir.dt.uint16
U8 = mybir.dt.uint8
FP8X4 = mybir.dt.float8_e4m3fn_x4
FP4X4 = mybir.dt.float4_e2m1fn_x4
ACT = mybir.ActivationFunctionType
ALU = mybir.AluOpType

P = 128
PACK = 4
PASSES = K // (P * PACK)
HALF = S // 2
CHUNK = 128
LN_03 = -1.2039728043259361
TINY = 2.0 ** -60
ON_VECTOR = ((3, 1),)


def tile_picked_yetasc_gate_p_kernel(
    tc, x_words, x_scales, w1_words, w1_scales, w2_words, w2_scales, load, unit, w3_words, w3_scales, offs, nxt, out
):
    nc = tc.nc
    with ExitStack() as ctx:
        sb = ctx.enter_context(tc.tile_pool(name="sb", bufs=1))
        ps = ctx.enter_context(tc.psum_pool(name="ps", bufs=1))

        def load_scale_rows(queue, plane, rows, quadrants):
            for q in quadrants:
                queue.dma_start(
                    out=plane[32 * q : 32 * q + 4, :, :].bitcast(I32),
                    in_=rows[:, 4 * q : 4 * q + 4, :].rearrange("o r n -> r o n").bitcast(I32),
                )

        offs_sb = sb.tile([P, S // 16], U16, name="offs_sb")
        nxt_sb = sb.tile([P, S // 16], U16, name="nxt_sb")
        x_bytes = sb.tile([P, PASSES, T], U8, name="x_bytes", align_bytes=64)
        x_table = sb.tile([P, PASSES, T], U32, name="x_table", align_bytes=64)
        ws_raw = sb.tile([P, 2, PASSES, H], U8, name="ws_raw", align_bytes=64)
        w3_sb = sb.tile([P, 2 * N], U8, name="w3_sb", align_bytes=64)
        w3s_sb = sb.tile([P, 1, N], U8, name="w3s_sb", align_bytes=64)
        load_sb = sb.tile([P, PACK, S], F32, name="load_sb")
        unit_sb = sb.tile([P, PACK], F32, name="unit_sb")

        nc.vector.memset(x_bytes[:, 0, :].bitcast(I32), 0)
        nc.gpsimd.memset(x_bytes[:, 1, :].bitcast(I32), 0)
        nc.vector.memset(ws_raw[:, 0].bitcast(I32), 0)
        nc.gpsimd.memset(ws_raw[:, 1].bitcast(I32), 0)
        nc.gpsimd.memset(w3s_sb[:].bitcast(I32), 0)

        def load_w(words, name):
            w_raw = sb.tile([P, PASSES, 2 * H], U8, name=name, align_bytes=64)
            nc.sync.dma_start(out=w_raw[:].bitcast(I32), in_=words.rearrange("o p n -> p o n").bitcast(I32))
            return w_raw

        xg = [sb.tile([P, S], U32, name="xg%d" % o, align_bytes=64) for o in range(PASSES)]
        xs = [sb.tile([P, S], U8, name="xs%d" % o, align_bytes=64) for o in range(PASSES)]
        wd = sb.tile([P, 2, PACK, PASSES, 2 * P], U8, name="wd", tag="wd", align_bytes=64)
        wsd = sb.tile([P, PACK, 2, PASSES, P], U8, name="wsd", align_bytes=64)

        def half_list(lst, h):
            return lst[:, h * (HALF // 16) : (h + 1) * (HALF // 16)]

        def deal_words(w_raw, i, t):
            src = w_raw[:].bitcast(U16).rearrange("p o (m t) -> p o t m", t=PACK)
            nc.scalar.copy(out=wd[:, i, t, :, :].bitcast(U16), in_=src[:, :, t, :])

        def deal_bytes(t):
            src = ws_raw[:].rearrange("p i o (m t) -> p t i o m", t=PACK)
            nc.gpsimd.tensor_copy(out=wsd[:, t], in_=src[:, t])

        nc.sync.dma_start(offs_sb[:], offs)
        w1_raw = load_w(w1_words, "w1_raw")
        load_scale_rows(nc.sync, x_bytes, x_scales, (0, 1))
        load_scale_rows(nc.scalar, x_bytes, x_scales, (2, 3))
        w2_raw = load_w(w2_words, "w2_raw")
        nc.sync.dma_start(out=x_table[:].bitcast(I32), in_=x_words.rearrange("o p n t -> p o (n t)").bitcast(I32))
        for i, rows in enumerate((w1_scales, w2_scales)):
            load_scale_rows(nc.sync, ws_raw[:, i], rows, range(3))
            load_scale_rows(nc.gpsimd, ws_raw[:, i], rows, (3,))
        nc.sync.dma_start(nxt_sb[:], nxt)
        load_rows = load.rearrange("(p t) j -> p t j", t=PACK)
        nc.sync.dma_start(out=unit_sb[:], in_=unit.rearrange("(p t) o -> p (t o)", t=PACK))
        for pair in range(2):
            nc.sync.dma_start(out=load_sb[:, 2 * pair : 2 * pair + 2, :], in_=load_rows[:, 2 * pair : 2 * pair + 2, :])
        nc.sync.dma_start(out=w3_sb[:].bitcast(I32), in_=w3_words[0].bitcast(I32))
        load_scale_rows(nc.sync, w3s_sb, w3_scales, range(4))

        for t in range(PACK):
            deal_words(w1_raw, 0, t)
        for t in range(PACK):
            deal_words(w2_raw, 1, t)
        for o in range(PASSES):
            nc.vector.tensor_copy(xs[o][:], x_bytes[:, o, :].indirect(offs_sb[:]))
        for h in range(2):
            for o in range(PASSES):
                nc.vector.tensor_copy(xg[o][:, h * HALF : (h + 1) * HALF], x_table[:, o, :].indirect(half_list(offs_sb, h)))
        for t in range(PACK):
            deal_bytes(t)

        sig = [sb.tile([P, S], F32, name="sig%d" % t) for t in range(PACK)]
        th = sb.tile([P, PACK, S], F32, name="th")
        rate = sb.tile([P, PACK, S], F32, name="rate")
        y_ps = {}

        def product(dst, i, t, cols):
            for o in range(PASSES):
                nc.tensor.matmul_mx(
                    out=dst,
                    lhsT=wd[:, i, t, o, :].bitcast(FP4X4),
                    lhsT_scale=wsd[:, t, i, o, :],
                    rhs=xg[o][:, cols].bitcast(FP8X4),
                    rhs_scale=xs[o][:, cols],
                    start=(o == 0),
                    stop=(o == PASSES - 1),
                )

        def rate_of(t, cols):
            nc.scalar.activation(out=rate[:, t, cols], in_=th[:, t, cols], func=ACT.Sigmoid, scale=-0.8, bias=LN_03)

        for h in range(2):
            cols = slice(h * HALF, (h + 1) * HALF)
            bank = ps.tile([P, 2, HALF], F32, name="first%d" % h, tag="first%d" % h)
            for i in range(2):
                product(bank[:, i, :], i, 0, cols)
            y_ps[(0, h)] = bank[:, 0, :]
            nc.scalar.activation(out=sig[0][:, cols], in_=bank[:, 0, :], func=ACT.Sigmoid)
            nc.scalar.activation(out=th[:, 0, cols], in_=bank[:, 1, :], func=ACT.Tanh)
            rate_of(0, cols)
        for t in range(1, PACK):
            tr_bank = ps.tile([P, S], F32, name="tr_bank%d" % t, tag="tr_bank%d" % t)
            y_bank = ps.tile([P, S], F32, name="y_bank%d" % t, tag="y_bank%d" % t)
            product(tr_bank[:], 1, t, slice(0, S))
            product(y_bank[:], 0, t, slice(0, S))
            for h in range(2):
                y_ps[(t, h)] = y_bank[:, h * HALF : (h + 1) * HALF]
            nc.scalar.activation(out=th[:, t, :], in_=tr_bank[:], func=ACT.Tanh)
            nc.scalar.activation(out=sig[t][:], in_=y_bank[:], func=ACT.Sigmoid)
            rate_of(t, slice(0, S))

        lsig = sb.tile([P, PACK, S], F32, name="lsig", tag="wd", align_bytes=64)
        soft = sb.tile([P, PACK, S], F32, name="soft")
        dw = [sb.tile([P, S], F32, name="dw%d" % t) for t in range(PACK)]
        dwn = sb.tile([P, PACK, S], F32, name="dwn")
        slow = sb.tile([P, PACK, S], F32, name="slow")
        lw = sb.tile([P, PACK, S], F32, name="lw")
        expo = sb.tile([P, PACK, S], F32, name="expo")
        sign_ = sb.tile([P, PACK, S], F32, name="sign_")
        gain = sb.tile([P, PACK, S], F32, name="gain")

        for t in range(PACK):
            nc.scalar.activation(out=lsig[:, t, :], in_=sig[t][:], func=ACT.Ln, bias=TINY)
        for t in range(PACK):
            for h in range(2):
                cols = slice(h * HALF, (h + 1) * HALF)
                nc.vector.tensor_tensor(soft[:, t, cols], lsig[:, t, cols], y_ps[(t, h)], ALU.subtract)
            for h in range(2):
                cols = slice(h * HALF, (h + 1) * HALF)
                nc.vector.tensor_tensor(dw[t][:, cols], soft[:, t, cols], rate[:, t, cols], ALU.mult)
            for h in range(2):
                cols = slice(h * HALF, (h + 1) * HALF)
                if (t, h) in ON_VECTOR:
                    nc.vector.tensor_copy(dwn[:, t, cols], dw[t][:].indirect(half_list(nxt_sb, h)))
                else:
                    nc.scalar.activation(out=dwn[:, t, cols], in_=dw[t][:].indirect(half_list(nxt_sb, h)), func=ACT.Copy)
        for t in range(PACK):
            nc.vector.scalar_tensor_tensor(slow[:, t, :], dwn[:, t, :], 0.0, dw[t][:], ALU.min, ALU.min)
            nc.scalar.activation(out=lw[:, t, :], in_=slow[:, t, :], func=ACT.Ln, scale=-1.0 / 0.3, bias=0.5)
        for t in range(PACK):
            nc.vector.scalar_tensor_tensor(expo[:, t, :], th[:, t, :], 0.8, lw[:, t, :], ALU.mult, ALU.subtract)
        for t in range(PACK):
            for h in range(2):
                cols = slice(h * HALF, (h + 1) * HALF)
                nc.vector.tensor_copy(sign_[:, t, cols], sig[t][:].indirect(half_list(nxt_sb, h)))
            nc.vector.scalar_tensor_tensor(gain[:, t, :], sign_[:, t, :], unit_sb[:, t : t + 1], load_sb[:, t, :], ALU.mult, ALU.mult)

        out_rows = out.rearrange("(u p) j -> p u j", p=P)
        for c in range(S // CHUNK):
            cols = slice(c * CHUNK, (c + 1) * CHUNK)
            ex = sb.tile([P, PACK, CHUNK], F32, name="ex%d" % c)
            woven = sb.tile([P, CHUNK, PACK], BF16, name="woven%d" % c, align_bytes=64)
            codes = sb.tile([P, CHUNK], U32, name="codes%d" % c, align_bytes=64)
            cs = sb.tile([P, CHUNK], U8, name="cs%d" % c, align_bytes=64)
            res = sb.tile([P, 2, CHUNK], F32, name="res%d" % c)
            acc = ps.tile([P, 2, CHUNK], F32, name="acc%d" % c, tag="tr_bank%d" % c if c else "first0")
            nc.scalar.activation(out=ex[:], in_=expo[:, :, cols], func=ACT.Exp)
            nc.vector.tensor_tensor(
                woven[:].rearrange("p (c i) t -> p c t i", i=4),
                ex[:].rearrange("p t (c i) -> p c t i", i=4),
                gain[:, :, cols].rearrange("p t (c i) -> p c t i", i=4),
                ALU.mult,
            )
            nc.vector.quantize_mx(out=codes[:].bitcast(FP8X4), scales=cs[:], in_=woven[:].rearrange("p j t -> p (j t)"))
            for u in range(2):
                nc.tensor.matmul_mx(
                    out=acc[:, u, :],
                    lhsT=w3_sb[:, u * 2 * P : (u + 1) * 2 * P].bitcast(FP4X4),
                    lhsT_scale=w3s_sb[:, 0, u * P : (u + 1) * P],
                    rhs=codes[:].bitcast(FP8X4),
                    rhs_scale=cs[:],
                    start=True,
                    stop=True,
                )
            nc.scalar.copy(out=res[:], in_=acc[:])
            nc.sync.dma_start(out=out_rows[:, :, cols], in_=res[:])
